import numpy as np
import ml_dtypes


def mxq(x, axis, fmt="e4m3"):
    dtype, down = {"e4m3": (ml_dtypes.float8_e4m3fn, 7), "e5m2": (ml_dtypes.float8_e5m2, 14)}[fmt]
    v = np.moveaxis(np.asarray(x, np.float32).astype(ml_dtypes.bfloat16).astype(np.float64), axis, -1)
    blocks = v.reshape(v.shape[:-1] + (-1, 32))
    amax = np.abs(blocks).max(-1, keepdims=True)
    byte = np.maximum(np.where(amax > 0, np.frexp(amax)[1] - 1 + 127, 0) - down, 1)
    scale = np.exp2(byte - 127.0)
    codes = (blocks / scale).astype(np.float32).astype(dtype).astype(np.float64)
    return np.moveaxis((codes * scale).reshape(v.shape), -1, axis)


WIDE = False


def mx_kscale(k):
    if not WIDE:
        return np.ones(k)
    levels = np.array([10, -10, 5, -5, 0])
    if k % 512:
        return np.exp2(np.random.permutation(np.resize(levels, k // 32))).repeat(32)
    a = np.empty((k // 512, 16))
    for p in range(k // 512):
        a[p, :8] = np.random.permutation(np.resize(levels, 8))
        for g in range(8):
            far = levels[np.abs(levels - a[p, g]) >= 10]
            a[p, g + 8] = far[np.random.randint(len(far))]
    return np.exp2(a.ravel()).repeat(32)


def f64(x):
    return np.asarray(x).astype(np.float64)


def striped(idx):
    return np.tile(idx.reshape(-1, 16).T, (8, 1)).astype(np.uint16)


def unstriped(offs):
    return offs[:16].T.reshape(-1).astype(np.int64)


def striped8(idx):
    return np.concatenate([x.reshape(-1, 16).T for x in idx]).astype(np.uint16)


def runs(offs, k):
    lists = np.stack([offs[16 * r : 16 * r + 16].T.reshape(-1) for r in range(8)]).astype(np.int64)
    return lists[np.arange(k) % 512 // 64]


def pack_weight(w):
    k, n = w.shape
    w = f64(np.asarray(w, np.float32).astype(ml_dtypes.bfloat16)).reshape(k // 32, 32, n)
    amax = np.abs(w).max(1)
    byte = np.clip(np.where(amax > 0, np.frexp(amax)[1] - 1 + 127 - 7, 1), 1, 254)
    scaled = (w * np.exp2(127.0 - byte)[:, None, :]).reshape(k, n).astype(np.float32)
    words = np.ascontiguousarray(scaled.reshape(k // 512, 128, 4, n).transpose(0, 1, 3, 2)).astype(ml_dtypes.float8_e4m3fn).view(np.uint8)
    return words, np.ascontiguousarray(byte.astype(np.uint8).reshape(k // 512, 16, n))


def unpack_weight(words, scales):
    g, p, n, _ = words.shape
    vals = np.ascontiguousarray(words).view(ml_dtypes.float8_e4m3fn).astype(np.float64) * np.repeat(np.exp2(scales.astype(np.float64) - 127.0), 8, axis=1)[..., None]
    return vals.transpose(0, 1, 3, 2).reshape(g * 512, n)


E2M1 = np.array([0.0, 0.5, 1.0, 1.5, 2.0, 3.0, 4.0, 6.0, -0.0, -0.5, -1.0, -1.5, -2.0, -3.0, -4.0, -6.0])


def pack_fp4(w):
    k, n = w.shape
    w = f64(np.asarray(w, np.float32).astype(ml_dtypes.bfloat16)).reshape(k // 32, 32, n)
    amax = np.abs(w).max(1)
    mant, ex = np.frexp(amax / 6.0)
    byte = np.clip(np.where(amax > 0, np.where(mant > 0.5, ex, ex - 1) + 127, 1), 1, 254)
    scaled = (w * np.exp2(127.0 - byte)[:, None, :]).reshape(k, n).astype(np.float32)
    c = np.ascontiguousarray(scaled.reshape(k // 512, 128, 4, n).transpose(0, 1, 3, 2)).astype(ml_dtypes.float4_e2m1fn).view(np.uint8) & 0xF
    words = (c[..., 0::2] | (c[..., 1::2] << 4)).reshape(k // 512, 128, 2 * n)
    return np.ascontiguousarray(words), np.ascontiguousarray(byte.astype(np.uint8).reshape(k // 512, 16, n))


def unpack_fp4(words, scales):
    g, _, n = scales.shape
    words = np.ascontiguousarray(words).reshape(g, 128, n, 2)
    nib = np.empty((g, 128, n, 4), np.uint8)
    nib[..., 0::2] = words & 0xF
    nib[..., 1::2] = words >> 4
    vals = E2M1[nib] * np.repeat(np.exp2(scales.astype(np.float64) - 127.0), 8, axis=1)[..., None]
    return vals.transpose(0, 1, 3, 2).reshape(g * 512, n)


def planes(y):
    n, m = y.shape
    v = y.astype(np.float32).astype(ml_dtypes.bfloat16).astype(np.float64).reshape(n // 32, 32, m)
    top = np.abs(v).max(1)
    byte = np.clip(np.where(top > 0, np.frexp(top)[1] - 1 + 127 - 7, 1), 1, 254)
    codes = (v * np.exp2(127.0 - byte)[:, None, :]).reshape(n, m).astype(np.float32).astype(ml_dtypes.float8_e4m3fn).view(np.uint8)
    words = codes.reshape(n // 512, 128, 4, m).transpose(0, 1, 3, 2)
    return np.ascontiguousarray(words), np.ascontiguousarray(byte.astype(np.uint8).reshape(n // 512, 16, m))


K, T, S, N, H, G, W = 512, 2048, 512, 512, 512, 2048, 256


def setup_inputs():
    n = np.random.standard_normal
    s = mx_kscale(K)[:, None]
    u = mx_kscale(S)
    packed_xT = pack_weight(n((K, T)) * s)
    packed_w1 = pack_fp4(n((K, H)) / np.sqrt(K) / s)
    packed_dT = pack_weight(n((K, G)) / s)
    packed_w2 = pack_fp4(n((H, N)) / np.sqrt(H) / u[:, None])
    perm = np.random.permutation(S)
    return {
        "x_words": packed_xT[0],
        "x_scales": packed_xT[1],
        "w1_words": packed_w1[0],
        "w1_scales": packed_w1[1],
        "d_words": packed_dT[0],
        "d_scales": packed_dT[1],
        "gn": (np.random.uniform(0.5, 1.5, (H, 1)) * u[:, None]).astype(np.float32),
        "w2_words": packed_w2[0],
        "w2_scales": packed_w2[1],
        "offs": striped(np.random.permutation(T)[:S]),
        "k1": striped8(np.random.randint(0, G, (8, H))),
        "two": striped(np.random.permutation(T)[:S]),
        "n1": striped(np.random.permutation(S)),
        "n2": striped(np.random.permutation(S)),
        "n3": striped(perm[:W]),
        "n4": striped(perm[W:]),
    }


def reference(x_words, x_scales, w1_words, w1_scales, d_words, d_scales, gn, w2_words, w2_scales, offs, k1, two, n1, n2, n3, n4):
    xq = unpack_weight(x_words, x_scales)[:, unstriped(offs)]
    y = unpack_fp4(w1_words, w1_scales).T @ xq
    d_k1 = unpack_weight(d_words, d_scales)[np.arange(K)[:, None], runs(k1, K)]
    x_two = unpack_weight(x_words, x_scales)[:, unstriped(two)]
    d = 0.0625 * (d_k1.T @ x_two)
    z = f64(gn) * (0.75 * (y * d[:, unstriped(n2)] - (y[:, unstriped(n1)] * d)))
    h = unpack_fp4(w2_words, w2_scales).T @ mxq(z, 0, "e4m3")
    pa = h[:, unstriped(n3)]
    pb = h[:, unstriped(n4)]
    rb = np.maximum(pa, pb)
    ra = pa / (np.abs(pb) + 0.5)
    ds = np.zeros((N, S))
    ds[:, unstriped(n3)] = ra
    out = ds.copy()
    out[:, unstriped(n4)] = rb
    return (out,) + planes(out)

@@ -1,0 +1,257 @@
+from contextlib import ExitStack
+
+import concourse.mybir as mybir
+
+K, T, S, N, H, G, W = 512, 2048, 512, 512, 512, 2048, 256
+FLOPS = 3 * 2 * 512 * 512 * 512
+
+F32 = mybir.dt.float32
+BF16 = mybir.dt.bfloat16
+I32 = mybir.dt.int32
+U32 = mybir.dt.uint32
+U16 = mybir.dt.uint16
+U8 = mybir.dt.uint8
+FP8X4 = mybir.dt.float8_e4m3fn_x4
+FP4X4 = mybir.dt.float4_e2m1fn_x4
+ALU = mybir.AluOpType
+ACT = mybir.ActivationFunctionType
+
+P = 128
+PACK = 4
+PIECES = ((0, 256), (256, 384), (384, 512))
+OUT_PIECES = ((0, 256), (256, 512))
+
+
+def tile_picked_twkeycrossbratio_none_po_kernel(tc, x_words, x_scales, w1_words, w1_scales, d_words, d_scales, gn, w2_words, w2_scales,
+        offs, k1, two, n1, n2, n3, n4, out_0, out_1, out_2):
+    nc = tc.nc
+    with ExitStack() as ctx:
+        lists = ctx.enter_context(tc.tile_pool(name="lists", bufs=1))
+        sb = ctx.enter_context(tc.tile_pool(name="sb", bufs=1))
+        ps = ctx.enter_context(tc.psum_pool(name="ps", bufs=1))
+
+        def tile(name, cols, dtype, tag=None):
+            return sb.tile([P, cols], dtype, name=name, tag=tag or name, align_bytes=64)
+
+        def load_list(name, src):
+            dst = lists.tile([P, src.shape[1]], U16, name=name)
+            nc.sync.dma_start(dst[:], src)
+            return dst
+
+        def load_plane(queue, dst, src):
+            for q in range(4):
+                queue.dma_start(dst[32 * q : 32 * q + 4, :].bitcast(I32), src[0, 4 * q : 4 * q + 4, :].bitcast(I32))
+
+        def words_of(src):
+            return src[0].rearrange("p c r -> p (c r)").bitcast(I32)
+
+        def gather_words(name, table, index, tag=None):
+            dst = tile(name, S, U32, tag)
+            nc.vector.tensor_copy(dst[:], table[:].bitcast(U32).indirect(index[:]))
+            return dst
+
+        def gather_bytes(name, table, index, tag=None):
+            dst = tile(name, S, U8, tag)
+            nc.vector.tensor_copy(dst[:], table[:].indirect(index[:]))
+            return dst
+
+        def deal(name, src, width):
+            dst = tile(name, src.shape[1], U8)
+            nc.vector.tensor_copy(
+                dst[:].rearrange("p (t m b) -> p t m b", t=PACK, b=width),
+                src[:].rearrange("p (m t b) -> p t m b", t=PACK, b=width),
+            )
+            return dst
+
+        xs = tile("xs", T, U8)
+        ds = tile("ds", G, U8)
+        w1s = tile("w1s", H, U8)
+        w2s = tile("w2s", N, U8)
+        dp_s = tile("dp_s", H, U8)
+        for plane in (xs, w1s, ds, w2s, dp_s):
+            nc.gpsimd.memset(plane[:].bitcast(I32), 0)
+        offs_l = load_list("offs_l", offs)
+        w1w = tile("w1w", 2 * H, U8, "staged")
+        nc.scalar.dma_start(w1w[:].bitcast(I32), w1_words[0].bitcast(I32))
+        k1_l = load_list("k1_l", k1)
+        w2w = tile("w2w", 2 * N, U8)
+        nc.scalar.dma_start(w2w[:].bitcast(I32), w2_words[0].bitcast(I32))
+        gain = tile("gain", PACK, F32)
+        nc.scalar.dma_start(gain[:], gn.rearrange("(p t) o -> p (t o)", t=PACK))
+        xw = tile("xw", T, I32)
+        nc.scalar.dma_start(xw[:], words_of(x_words))
+        load_plane(nc.sync, xs, x_scales)
+        nc.sync.dma_start(ds[0:P:8, :].bitcast(I32), d_scales[0].bitcast(I32))
+        load_plane(nc.sync, w1s, w1_scales)
+        w1w_d = deal("w1w_d", w1w, 2)
+        dw = tile("dw", G, I32, "staged")
+        nc.sync.dma_start(dw[:], words_of(d_words))
+        two_l = load_list("two_l", two)
+        n1_l = load_list("n1_l", n1)
+        n2_l = load_list("n2_l", n2)
+        n3_l = load_list("n3_l", n3)
+        n4_l = load_list("n4_l", n4)
+        load_plane(nc.gpsimd, w2s, w2_scales)
+
+
+        w2w_d = deal("w2w_d", w2w, 2)
+        xq_s = gather_bytes("xq_s", xs, offs_l, "token_bytes")
+        xq_w = gather_words("xq_w", xw, offs_l, "token_words")
+        w1s_d = deal("w1s_d", w1s, 1)
+        y_ps = [ps.tile([P, S], F32, name="bank%d" % t) for t in range(PACK)]
+        for t in range(PACK):
+            nc.tensor.matmul_mx(
+                out=y_ps[t][:],
+                lhsT=w1w_d[:, 2 * P * t : 2 * P * (t + 1)].bitcast(FP4X4),
+                lhsT_scale=w1s_d[:, P * t : P * (t + 1)],
+                rhs=xq_w[:].bitcast(FP8X4),
+                rhs_scale=xq_s[:],
+                start=True,
+                stop=True,
+            )
+        dg_s = gather_bytes("dg_s", ds, k1_l, "w1s")
+        dd_s = deal("dd_s", dg_s, 1)
+        for r in range(4):
+            nc.sync.dma_start(dp_s[r:P:32, :].bitcast(I32), dd_s[8 * r : P : 32, :].bitcast(I32))
+        dg_w = gather_words("dg_w", dw, k1_l)
+        dd_w = [tile("dd_w%d" % t, P, U32) for t in range(PACK)]
+        for t in range(PACK):
+            nc.vector.tensor_copy(dd_w[t][:], dg_w[:, t::PACK])
+        xt_w = gather_words("xt_w", xw, two_l, "token_words")
+        xt_s = gather_bytes("xt_s", xs, two_l, "token_bytes")
+        d_ps = [ps.tile([P, S], F32, name="bank%d" % (PACK + t)) for t in range(PACK)]
+        for t in range(PACK):
+            nc.tensor.matmul_mx(
+                out=d_ps[t][:],
+                lhsT=dd_w[t][:].bitcast(FP8X4),
+                lhsT_scale=dp_s[:, P * t : P * (t + 1)],
+                rhs=xt_w[:].bitcast(FP8X4),
+                rhs_scale=xt_s[:],
+                start=True,
+                stop=True,
+            )
+        w2s_d = deal("w2s_d", w2s, 1)
+        factor = tile("factor", PACK, F32)
+        nc.gpsimd.tensor_scalar(factor[:], gain[:], 0.75 * 0.0625, 0.0, ALU.mult, ALU.add)
+
+        def entries(index, lo, hi):
+            return index[:, lo // 16 : hi // 16]
+
+        y_sb = [tile("y_sb%d" % t, S, F32) for t in range(PACK)]
+        d_sb = [tile("d_sb%d" % t, S, F32) for t in range(PACK)]
+        early = (512, 512, 256, 256)
+        y_early = [tile("y_early%d" % t, early[t], F32) for t in range(PACK)]
+        for t in range(PACK):
+            nc.scalar.copy(y_sb[t][:], y_ps[t][:])
+            nc.scalar.activation(y_early[t][:], y_sb[t][:].indirect(entries(n1_l, 0, early[t])), ACT.Copy)
+        for t in range(PACK):
+            if t in (0,):
+                nc.vector.tensor_scalar(d_sb[t][:], d_ps[t][:], factor[:, t : t + 1], None, ALU.mult)
+            else:
+                nc.scalar.activation(d_sb[t][:], d_ps[t][:], ACT.Copy, scale=factor[:, t : t + 1])
+        y_late = tile("y_late", PACK * S, F32, "token_words")
+        d_n2 = tile("d_n2", PACK * S, F32)
+        fused = ((0, 0), (1, 0))
+        for u, (lo, hi) in enumerate(PIECES):
+            for t in range(PACK):
+                if lo >= early[t]:
+                    nc.scalar.activation(y_late[:, S * t + lo : S * t + hi], y_sb[t][:].indirect(entries(n1_l, lo, hi)), ACT.Copy)
+                if (t, u) not in fused:
+                    nc.scalar.activation(d_n2[:, S * t + lo : S * t + hi], d_sb[t][:].indirect(entries(n2_l, lo, hi)), ACT.Copy)
+
+        h_ps = [ps.tile([P, S], F32, name="bank%d" % t) for t in range(PACK)]
+        h_sb = [tile("h_sb%d" % t, S, F32) for t in range(PACK)]
+        for u, (lo, hi) in enumerate(PIECES):
+            width = hi - lo
+            left = tile("left%d" % u, PACK * width, F32)
+            right = tile("right%d" % u, PACK * width, F32)
+            for t in range(PACK):
+                mine = slice(t * width, (t + 1) * width)
+                y_n1 = y_early[t][:, lo:hi] if lo < early[t] else y_late[:, S * t + lo : S * t + hi]
+                nc.vector.tensor_tensor(right[:, mine], y_n1, d_sb[t][:, lo:hi], ALU.mult)
+                if (t, u) in fused:
+                    looked = d_sb[t][:].indirect(entries(n2_l, lo, hi))
+                else:
+                    looked = d_n2[:, S * t + lo : S * t + hi]
+                nc.vector.tensor_tensor(left[:, mine], looked, y_sb[t][:, lo:hi], ALU.mult)
+            z = tile("z%d" % u, PACK * width, BF16)
+            nc.vector.tensor_tensor(
+                z[:].rearrange("p (c i t) -> p c t i", i=4, t=PACK),
+                left[:].rearrange("p (t c i) -> p c t i", i=4, t=PACK),
+                right[:].rearrange("p (t c i) -> p c t i", i=4, t=PACK),
+                ALU.subtract,
+            )
+            z_w = tile("z_w%d" % u, width, U32)
+            z_s = tile("z_s%d" % u, width, U8)
+            nc.vector.quantize_mx(out=z_w[:].bitcast(FP8X4), scales=z_s[:], in_=z[:])
+            for t in range(PACK):
+                nc.tensor.matmul_mx(
+                    out=h_ps[t][:, lo:hi],
+                    lhsT=w2w_d[:, 2 * P * t : 2 * P * (t + 1)].bitcast(FP4X4),
+                    lhsT_scale=w2s_d[:, P * t : P * (t + 1)],
+                    rhs=z_w[:].bitcast(FP8X4),
+                    rhs_scale=z_s[:],
+                    start=True,
+                    stop=True,
+                )
+                if (t, u) in ((1, 2), (3, 2)):
+                    nc.vector.tensor_copy(h_sb[t][:, lo:hi], h_ps[t][:, lo:hi])
+                else:
+                    nc.scalar.copy(h_sb[t][:, lo:hi], h_ps[t][:, lo:hi])
+
+        def part(t):
+            return slice(t * W, (t + 1) * W)
+
+        out_rows = out_0.rearrange("(p t) c -> p t c", t=PACK)
+        pa = tile("pa", PACK * W, F32)
+        pb = tile("pb", PACK * W, F32)
+        size = tile("size", PACK * W, F32)
+        root = tile("root", PACK * W, F32)
+        inv = tile("inv", PACK * W, F32)
+        rb = tile("rb", PACK * W, F32)
+        ra = tile("ra", 2 * W, F32)
+        res = [tile("res%d" % t, S, F32) for t in range(PACK)]
+        for t in range(PACK):
+            nc.scalar.activation(pb[:, part(t)], h_sb[t][:].indirect(n4_l[:]), ACT.Copy)
+            nc.vector.tensor_copy(pa[:, part(t)], h_sb[t][:].indirect(n3_l[:]))
+        sides = (slice(0, 2 * W), slice(2 * W, 4 * W))
+        for side in sides:
+            nc.scalar.activation(size[:, side], pb[:, side], ACT.Abs)
+        for side in sides:
+            nc.scalar.activation(root[:, side], size[:, side], ACT.Abs_reciprocal_sqrt, bias=0.5)
+        for side in sides:
+            nc.scalar.activation(inv[:, side], root[:, side], ACT.Square)
+        for side in sides:
+            nc.vector.tensor_tensor(rb[:, side], pa[:, side], pb[:, side], ALU.max)
+        nc.vector.tensor_tensor(ra[:], pa[:, sides[0]], inv[:, sides[0]], ALU.mult)
+        for t in range(PACK):
+            if t >= 2:
+                nc.vector.tensor_copy(res[t][:].indirect(n4_l[:]), rb[:, part(t)])
+            else:
+                nc.scalar.activation(res[t][:].indirect(n4_l[:]), rb[:, part(t)], ACT.Copy)
+        for t in range(PACK):
+            if t >= 2:
+                nc.vector.tensor_tensor(res[t][:].indirect(n3_l[:]), pa[:, part(t)], inv[:, part(t)], ALU.mult)
+            else:
+                nc.scalar.activation(res[t][:].indirect(n3_l[:]), ra[:, part(t)], ACT.Copy)
+            nc.sync.dma_start(out_rows[:, t, :], res[t][:])
+        pairs = [tile("pairs%d" % u, PACK * (hi - lo), BF16) for u, (lo, hi) in enumerate(OUT_PIECES)]
+        for t in (2, 3, 0, 1):
+            for u, (lo, hi) in enumerate(OUT_PIECES):
+                nc.vector.tensor_copy(
+                    pairs[u][:].rearrange("p (v c e) -> p v c e", v=2, e=2)[:, t // 2, :, t % 2], res[t][:, lo:hi]
+                )
+        grouped = [tile("grouped%d" % u, PACK * (hi - lo), BF16) for u, (lo, hi) in enumerate(OUT_PIECES)]
+        for u in range(len(OUT_PIECES)):
+            nc.vector.tensor_copy(
+                grouped[u][:].bitcast(I32).rearrange("p (c i v) -> p c v i", v=2, i=4),
+                pairs[u][:].bitcast(I32).rearrange("p (v c i) -> p c v i", v=2, i=4),
+            )
+        o_w = tile("o_w", S, I32)
+        o_s = tile("o_s", S, U8)
+        for u, (lo, hi) in enumerate(OUT_PIECES):
+            nc.vector.quantize_mx(out=o_w[:, lo:hi].bitcast(FP8X4), scales=o_s[:, lo:hi], in_=grouped[u][:])
+            nc.sync.dma_start(words_of(out_1)[:, lo:hi], o_w[:, lo:hi])
+        for q in range(4):
+            queue = nc.scalar if q % 2 == 0 else nc.sync
+            queue.dma_start(out_2[0, 4 * q : 4 * q + 4, :].bitcast(I32), o_s[32 * q : 32 * q + 4, :].bitcast(I32))

@@ -55,8 +55,8 @@ def tile_picked_twkeycrossbratio_none_po_kernel(tc, x_words, x_scales, w1_words,
             nc.vector.tensor_copy(dst[:], table[:].indirect(index[:]))
             return dst
 
-        def deal(name, src, width):
-            dst = tile(name, src.shape[1], U8)
+        def deal(name, src, width, tag=None):
+            dst = tile(name, src.shape[1], U8, tag)
             nc.vector.tensor_copy(
                 dst[:].rearrange("p (t m b) -> p t m b", t=PACK, b=width),
                 src[:].rearrange("p (m t b) -> p t m b", t=PACK, b=width),
@@ -68,31 +68,38 @@ def tile_picked_twkeycrossbratio_none_po_kernel(tc, x_words, x_scales, w1_words,
         w1s = tile("w1s", H, U8)
         w2s = tile("w2s", N, U8)
         dp_s = tile("dp_s", H, U8)
-        for plane in (xs, w1s, ds, w2s, dp_s):
+        nc.gpsimd.memset(xs[:, : T // 2].bitcast(I32), 0)
+        nc.vector.memset(xs[:, T // 2 :].bitcast(I32), 0)
+        for plane in (w1s, ds, w2s, dp_s):
             nc.gpsimd.memset(plane[:].bitcast(I32), 0)
+
         offs_l = load_list("offs_l", offs)
         w1w = tile("w1w", 2 * H, U8, "staged")
-        nc.scalar.dma_start(w1w[:].bitcast(I32), w1_words[0].bitcast(I32))
-        k1_l = load_list("k1_l", k1)
+        nc.sync.dma_start(w1w[:].bitcast(I32), w1_words[0].bitcast(I32))
         w2w = tile("w2w", 2 * N, U8)
-        nc.scalar.dma_start(w2w[:].bitcast(I32), w2_words[0].bitcast(I32))
-        gain = tile("gain", PACK, F32)
-        nc.scalar.dma_start(gain[:], gn.rearrange("(p t) o -> p (t o)", t=PACK))
-        xw = tile("xw", T, I32)
-        nc.scalar.dma_start(xw[:], words_of(x_words))
+        nc.sync.dma_start(w2w[:].bitcast(I32), w2_words[0].bitcast(I32))
         load_plane(nc.sync, xs, x_scales)
-        nc.sync.dma_start(ds[0:P:8, :].bitcast(I32), d_scales[0].bitcast(I32))
+        xw = tile("xw", T, I32)
+        nc.sync.dma_start(xw[:], words_of(x_words))
         load_plane(nc.sync, w1s, w1_scales)
+        nc.sync.dma_start(ds[0:P:8, :].bitcast(I32), d_scales[0].bitcast(I32))
+        k1_l = load_list("k1_l", k1)
+        n1_l = load_list("n1_l", n1)
         w1w_d = deal("w1w_d", w1w, 2)
         dw = tile("dw", G, I32, "staged")
         nc.sync.dma_start(dw[:], words_of(d_words))
         two_l = load_list("two_l", two)
-        n1_l = load_list("n1_l", n1)
         n2_l = load_list("n2_l", n2)
+        gain = tile("gain", PACK, F32)
+        nc.sync.dma_start(gain[:], gn.rearrange("(p t) o -> p (t o)", t=PACK))
+        load_plane(nc.sync, w2s, w2_scales)
         n3_l = load_list("n3_l", n3)
         n4_l = load_list("n4_l", n4)
-        load_plane(nc.gpsimd, w2s, w2_scales)
 
+        warm_in = tile("warm_in", 1, F32)
+        warm = tile("warm", 1, F32)
+        nc.gpsimd.memset(warm_in[:], 1.0)
+        nc.scalar.activation(warm[:], warm_in[:], ACT.Abs_reciprocal_sqrt)
 
         w2w_d = deal("w2w_d", w2w, 2)
         xq_s = gather_bytes("xq_s", xs, offs_l, "token_bytes")
@@ -114,23 +121,22 @@ def tile_picked_twkeycrossbratio_none_po_kernel(tc, x_words, x_scales, w1_words,
         for r in range(4):
             nc.sync.dma_start(dp_s[r:P:32, :].bitcast(I32), dd_s[8 * r : P : 32, :].bitcast(I32))
         dg_w = gather_words("dg_w", dw, k1_l)
-        dd_w = [tile("dd_w%d" % t, P, U32) for t in range(PACK)]
-        for t in range(PACK):
-            nc.vector.tensor_copy(dd_w[t][:], dg_w[:, t::PACK])
+        dd_w = tile("dd_w", H, U32)
+        nc.vector.tensor_copy(dd_w[:].rearrange("p (t m) -> p m t", t=PACK), dg_w[:].rearrange("p (m t) -> p m t", t=PACK))
         xt_w = gather_words("xt_w", xw, two_l, "token_words")
         xt_s = gather_bytes("xt_s", xs, two_l, "token_bytes")
         d_ps = [ps.tile([P, S], F32, name="bank%d" % (PACK + t)) for t in range(PACK)]
         for t in range(PACK):
             nc.tensor.matmul_mx(
                 out=d_ps[t][:],
-                lhsT=dd_w[t][:].bitcast(FP8X4),
+                lhsT=dd_w[:, P * t : P * (t + 1)].bitcast(FP8X4),
                 lhsT_scale=dp_s[:, P * t : P * (t + 1)],
                 rhs=xt_w[:].bitcast(FP8X4),
                 rhs_scale=xt_s[:],
                 start=True,
                 stop=True,
             )
-        w2s_d = deal("w2s_d", w2s, 1)
+        w2s_d = deal("w2s_d", w2s, 1, "dg_w")
         factor = tile("factor", PACK, F32)
         nc.gpsimd.tensor_scalar(factor[:], gain[:], 0.75 * 0.0625, 0.0, ALU.mult, ALU.add)
 
@@ -143,7 +149,8 @@ def tile_picked_twkeycrossbratio_none_po_kernel(tc, x_words, x_scales, w1_words,
         y_early = [tile("y_early%d" % t, early[t], F32) for t in range(PACK)]
         for t in range(PACK):
             nc.scalar.copy(y_sb[t][:], y_ps[t][:])
-            nc.scalar.activation(y_early[t][:], y_sb[t][:].indirect(entries(n1_l, 0, early[t])), ACT.Copy)
+            for lo in range(0, early[t], W):
+                nc.scalar.activation(y_early[t][:, lo : lo + W], y_sb[t][:].indirect(entries(n1_l, lo, lo + W)), ACT.Copy)
         for t in range(PACK):
             if t in (0,):
                 nc.vector.tensor_scalar(d_sb[t][:], d_ps[t][:], factor[:, t : t + 1], None, ALU.mult)
@@ -244,8 +251,8 @@ def tile_picked_twkeycrossbratio_none_po_kernel(tc, x_words, x_scales, w1_words,
         grouped = [tile("grouped%d" % u, PACK * (hi - lo), BF16) for u, (lo, hi) in enumerate(OUT_PIECES)]
         for u in range(len(OUT_PIECES)):
             nc.vector.tensor_copy(
-                grouped[u][:].bitcast(I32).rearrange("p (c i v) -> p c v i", v=2, i=4),
-                pairs[u][:].bitcast(I32).rearrange("p (v c i) -> p c v i", v=2, i=4),
+                grouped[u][:].bitcast(I32).rearrange("p (c v) -> p c v", v=2),
+                pairs[u][:].bitcast(I32).rearrange("p (v c) -> p c v", v=2),
             )
         o_w = tile("o_w", S, I32)
         o_s = tile("o_s", S, U8)

@@ -66,11 +66,10 @@ def tile_picked_twkeycrossbratio_none_po_kernel(tc, x_words, x_scales, w1_words,
         xs = tile("xs", T, U8)
         ds = tile("ds", G, U8)
         w1s = tile("w1s", H, U8)
-        w2s = tile("w2s", N, U8)
         dp_s = tile("dp_s", H, U8)
         nc.gpsimd.memset(xs[:, : T // 2].bitcast(I32), 0)
         nc.vector.memset(xs[:, T // 2 :].bitcast(I32), 0)
-        for plane in (w1s, ds, w2s, dp_s):
+        for plane in (w1s, ds, dp_s):
             nc.gpsimd.memset(plane[:].bitcast(I32), 0)
 
         offs_l = load_list("offs_l", offs)
@@ -84,15 +83,14 @@ def tile_picked_twkeycrossbratio_none_po_kernel(tc, x_words, x_scales, w1_words,
         load_plane(nc.sync, w1s, w1_scales)
         nc.sync.dma_start(ds[0:P:8, :].bitcast(I32), d_scales[0].bitcast(I32))
         k1_l = load_list("k1_l", k1)
-        n1_l = load_list("n1_l", n1)
+        two_l = load_list("two_l", two)
         w1w_d = deal("w1w_d", w1w, 2)
         dw = tile("dw", G, I32, "staged")
         nc.sync.dma_start(dw[:], words_of(d_words))
-        two_l = load_list("two_l", two)
+        n1_l = load_list("n1_l", n1)
         n2_l = load_list("n2_l", n2)
         gain = tile("gain", PACK, F32)
         nc.sync.dma_start(gain[:], gn.rearrange("(p t) o -> p (t o)", t=PACK))
-        load_plane(nc.sync, w2s, w2_scales)
         n3_l = load_list("n3_l", n3)
         n4_l = load_list("n4_l", n4)
 
@@ -101,110 +99,110 @@ def tile_picked_twkeycrossbratio_none_po_kernel(tc, x_words, x_scales, w1_words,
         nc.gpsimd.memset(warm_in[:], 1.0)
         nc.scalar.activation(warm[:], warm_in[:], ACT.Abs_reciprocal_sqrt)
 
-        w2w_d = deal("w2w_d", w2w, 2)
-        xq_s = gather_bytes("xq_s", xs, offs_l, "token_bytes")
-        xq_w = gather_words("xq_w", xw, offs_l, "token_words")
-        w1s_d = deal("w1s_d", w1s, 1)
-        y_ps = [ps.tile([P, S], F32, name="bank%d" % t) for t in range(PACK)]
-        for t in range(PACK):
-            nc.tensor.matmul_mx(
-                out=y_ps[t][:],
-                lhsT=w1w_d[:, 2 * P * t : 2 * P * (t + 1)].bitcast(FP4X4),
-                lhsT_scale=w1s_d[:, P * t : P * (t + 1)],
-                rhs=xq_w[:].bitcast(FP8X4),
-                rhs_scale=xq_s[:],
-                start=True,
-                stop=True,
-            )
-        dg_s = gather_bytes("dg_s", ds, k1_l, "w1s")
-        dd_s = deal("dd_s", dg_s, 1)
-        for r in range(4):
-            nc.sync.dma_start(dp_s[r:P:32, :].bitcast(I32), dd_s[8 * r : P : 32, :].bitcast(I32))
-        dg_w = gather_words("dg_w", dw, k1_l)
-        dd_w = tile("dd_w", H, U32)
-        nc.vector.tensor_copy(dd_w[:].rearrange("p (t m) -> p m t", t=PACK), dg_w[:].rearrange("p (m t) -> p m t", t=PACK))
-        xt_w = gather_words("xt_w", xw, two_l, "token_words")
-        xt_s = gather_bytes("xt_s", xs, two_l, "token_bytes")
-        d_ps = [ps.tile([P, S], F32, name="bank%d" % (PACK + t)) for t in range(PACK)]
-        for t in range(PACK):
-            nc.tensor.matmul_mx(
-                out=d_ps[t][:],
-                lhsT=dd_w[:, P * t : P * (t + 1)].bitcast(FP8X4),
-                lhsT_scale=dp_s[:, P * t : P * (t + 1)],
-                rhs=xt_w[:].bitcast(FP8X4),
-                rhs_scale=xt_s[:],
-                start=True,
-                stop=True,
-            )
-        w2s_d = deal("w2s_d", w2s, 1, "dg_w")
-        factor = tile("factor", PACK, F32)
-        nc.gpsimd.tensor_scalar(factor[:], gain[:], 0.75 * 0.0625, 0.0, ALU.mult, ALU.add)
+        halves = ((0, W), (W, S))
 
         def entries(index, lo, hi):
             return index[:, lo // 16 : hi // 16]
 
+        def product(out, lhsT, lhsT_scale, rhs, rhs_scale):
+            nc.tensor.matmul_mx(out=out, lhsT=lhsT, lhsT_scale=lhsT_scale, rhs=rhs, rhs_scale=rhs_scale, start=True, stop=True)
+
+        w2w_d = deal("w2w_d", w2w, 2)
+        xq_s = gather_bytes("xq_s", xs, offs_l, "token_bytes")
         y_sb = [tile("y_sb%d" % t, S, F32) for t in range(PACK)]
-        d_sb = [tile("d_sb%d" % t, S, F32) for t in range(PACK)]
-        early = (512, 512, 256, 256)
-        y_early = [tile("y_early%d" % t, early[t], F32) for t in range(PACK)]
-        for t in range(PACK):
-            nc.scalar.copy(y_sb[t][:], y_ps[t][:])
-            for lo in range(0, early[t], W):
-                nc.scalar.activation(y_early[t][:, lo : lo + W], y_sb[t][:].indirect(entries(n1_l, lo, lo + W)), ACT.Copy)
-        for t in range(PACK):
-            if t in (0,):
-                nc.vector.tensor_scalar(d_sb[t][:], d_ps[t][:], factor[:, t : t + 1], None, ALU.mult)
-            else:
-                nc.scalar.activation(d_sb[t][:], d_ps[t][:], ACT.Copy, scale=factor[:, t : t + 1])
-        y_late = tile("y_late", PACK * S, F32, "token_words")
-        d_n2 = tile("d_n2", PACK * S, F32)
-        fused = ((0, 0), (1, 0))
-        for u, (lo, hi) in enumerate(PIECES):
+        w1s_d = deal("w1s_d", w1s, 1)
+        for u, (lo, hi) in enumerate(halves):
+            xq_w = tile("xq_w%d" % u, W, U32, "token_words%d" % u)
+            nc.vector.tensor_copy(xq_w[:], xw[:].bitcast(U32).indirect(entries(offs_l, lo, hi)))
             for t in range(PACK):
-                if lo >= early[t]:
+                y_ps = ps.tile([P, W], F32, name="bank%d" % (PACK * u + t))
+                product(y_ps[:], w1w_d[:, 2 * P * t : 2 * P * (t + 1)].bitcast(FP4X4), w1s_d[:, P * t : P * (t + 1)],
+                        xq_w[:].bitcast(FP8X4), xq_s[:, lo:hi])
+                nc.scalar.copy(y_sb[t][:, lo:hi], y_ps[:])
+        y_n1 = {}
+
+        def fetch_y(t, u, dst):
+            y_n1[t, u] = dst
+            nc.scalar.activation(dst, y_sb[t][:].indirect(entries(n1_l, *halves[u])), ACT.Copy)
+
+        early = 4
+        y_early = tile("y_early", early * W, F32)
+        for e in range(early):
+            fetch_y(e % PACK, e // PACK, y_early[:, e * W : (e + 1) * W])
+        dg_s = gather_bytes("dg_s", ds, k1_l, "w1s")
+        dd_s = deal("dd_s", dg_s, 1)
+        for r in range(4):
+            nc.sync.dma_start(dp_s[r:P:32, :].bitcast(I32), dd_s[8 * r : P : 32, :].bitcast(I32))
+        w2s = tile("w2s", N, U8, "dd_s")
+        nc.gpsimd.memset(w2s[:].bitcast(I32), 0)
+        load_plane(nc.sync, w2s, w2_scales)
+        dg_w = gather_words("dg_w", dw, k1_l)
+        dd_w = tile("dd_w", H, U32)
+        nc.vector.tensor_copy(dd_w[:].rearrange("p (t m) -> p m t", t=PACK), dg_w[:].rearrange("p (m t) -> p m t", t=PACK))
+        factor = tile("factor", PACK, F32)
+        nc.gpsimd.tensor_scalar(factor[:], gain[:], 0.75 * 0.0625, 0.0, ALU.mult, ALU.add)
+        d_sb = [tile("d_sb%d" % t, S, F32) for t in range(PACK)]
+        for u, (lo, hi) in enumerate(halves):
+            xt_w = tile("xt_w%d" % u, W, U32, ("token_words0", "dg_w")[u])
+            xt_s = tile("xt_s%d" % u, W, U8, ("token_bytes", "staged")[u])
+            nc.vector.tensor_copy(xt_w[:], xw[:].bitcast(U32).indirect(entries(two_l, lo, hi)))
+            nc.vector.tensor_copy(xt_s[:], xs[:].indirect(entries(two_l, lo, hi)))
+            for t in range(PACK):
+                d_ps = ps.tile([P, W], F32, name="bank%d" % (PACK * u + t))
+                product(d_ps[:], dd_w[:, P * t : P * (t + 1)].bitcast(FP8X4), dp_s[:, P * t : P * (t + 1)],
+                        xt_w[:].bitcast(FP8X4), xt_s[:])
+                nc.scalar.activation(d_sb[t][:, lo:hi], d_ps[:], ACT.Copy, scale=factor[:, t : t + 1])
+        w2s_d = deal("w2s_d", w2s, 1)
+
+        y_late = tile("y_late", PACK * S, F32, "dg_w")
+        d_n2 = tile("d_n2", PACK * S, F32)
+        fused = 4
+        spans = ((0, 256), (256, 512))
+        for lo, hi in spans:
+            for t in range(PACK):
+                if lo >= W:
                     nc.scalar.activation(y_late[:, S * t + lo : S * t + hi], y_sb[t][:].indirect(entries(n1_l, lo, hi)), ACT.Copy)
-                if (t, u) not in fused:
+                if not (lo == 0 and t < fused):
                     nc.scalar.activation(d_n2[:, S * t + lo : S * t + hi], d_sb[t][:].indirect(entries(n2_l, lo, hi)), ACT.Copy)
 
-        h_ps = [ps.tile([P, S], F32, name="bank%d" % t) for t in range(PACK)]
         h_sb = [tile("h_sb%d" % t, S, F32) for t in range(PACK)]
-        for u, (lo, hi) in enumerate(PIECES):
+        for lo, hi in spans:
             width = hi - lo
-            left = tile("left%d" % u, PACK * width, F32)
-            right = tile("right%d" % u, PACK * width, F32)
+            left = tile("left%d" % lo, PACK * width, F32)
+            right = tile("right%d" % lo, PACK * width, F32)
             for t in range(PACK):
-                mine = slice(t * width, (t + 1) * width)
-                y_n1 = y_early[t][:, lo:hi] if lo < early[t] else y_late[:, S * t + lo : S * t + hi]
-                nc.vector.tensor_tensor(right[:, mine], y_n1, d_sb[t][:, lo:hi], ALU.mult)
-                if (t, u) in fused:
+                y_at = y_n1[t, 0] if lo == 0 else y_late[:, S * t + lo : S * t + hi]
+                nc.vector.tensor_tensor(right[:, width * t : width * (t + 1)], y_at, d_sb[t][:, lo:hi], ALU.mult)
+            for t in range(PACK):
+                if lo == 0 and t < fused:
                     looked = d_sb[t][:].indirect(entries(n2_l, lo, hi))
                 else:
                     looked = d_n2[:, S * t + lo : S * t + hi]
-                nc.vector.tensor_tensor(left[:, mine], looked, y_sb[t][:, lo:hi], ALU.mult)
-            z = tile("z%d" % u, PACK * width, BF16)
-            nc.vector.tensor_tensor(
-                z[:].rearrange("p (c i t) -> p c t i", i=4, t=PACK),
-                left[:].rearrange("p (t c i) -> p c t i", i=4, t=PACK),
-                right[:].rearrange("p (t c i) -> p c t i", i=4, t=PACK),
-                ALU.subtract,
-            )
-            z_w = tile("z_w%d" % u, width, U32)
-            z_s = tile("z_s%d" % u, width, U8)
-            nc.vector.quantize_mx(out=z_w[:].bitcast(FP8X4), scales=z_s[:], in_=z[:])
-            for t in range(PACK):
-                nc.tensor.matmul_mx(
-                    out=h_ps[t][:, lo:hi],
-                    lhsT=w2w_d[:, 2 * P * t : 2 * P * (t + 1)].bitcast(FP4X4),
-                    lhsT_scale=w2s_d[:, P * t : P * (t + 1)],
-                    rhs=z_w[:].bitcast(FP8X4),
-                    rhs_scale=z_s[:],
-                    start=True,
-                    stop=True,
+                nc.vector.tensor_tensor(left[:, width * t : width * (t + 1)], looked, y_sb[t][:, lo:hi], ALU.mult)
+            pieces = [(a, b) for a, b in PIECES if lo <= a < hi]
+            z = {}
+            for a, b in pieces:
+                z[a] = tile("z%d" % a, PACK * (b - a), BF16)
+                cols = slice((a - lo) // 4, (b - lo) // 4)
+                nc.vector.tensor_tensor(
+                    z[a][:].rearrange("p (c i t) -> p c t i", i=4, t=PACK),
+                    left[:].rearrange("p (t c i) -> p c t i", i=4, t=PACK)[:, cols],
+                    right[:].rearrange("p (t c i) -> p c t i", i=4, t=PACK)[:, cols],
+                    ALU.subtract,
                 )
-                if (t, u) in ((1, 2), (3, 2)):
-                    nc.vector.tensor_copy(h_sb[t][:, lo:hi], h_ps[t][:, lo:hi])
-                else:
-                    nc.scalar.copy(h_sb[t][:, lo:hi], h_ps[t][:, lo:hi])
+            for a, b in pieces:
+                z_w = tile("z_w%d" % a, b - a, U32)
+                z_s = tile("z_s%d" % a, b - a, U8)
+                nc.vector.quantize_mx(out=z_w[:].bitcast(FP8X4), scales=z_s[:], in_=z[a][:])
+                first_bank = PACK * (PIECES.index((a, b)) % 2)
+                h_ps = [ps.tile([P, b - a], F32, name="bank%d" % (first_bank + t)) for t in range(PACK)]
+                for t in range(PACK):
+                    product(h_ps[t][:], w2w_d[:, 2 * P * t : 2 * P * (t + 1)].bitcast(FP4X4), w2s_d[:, P * t : P * (t + 1)],
+                            z_w[:].bitcast(FP8X4), z_s[:])
+                    if a >= 256 and t % 2 == 1:
+                        nc.vector.tensor_copy(h_sb[t][:, a:b], h_ps[t][:])
+                    else:
+                        nc.scalar.copy(h_sb[t][:, a:b], h_ps[t][:])
 
         def part(t):
             return slice(t * W, (t + 1) * W)

@@ -2,7 +2,7 @@ from contextlib import ExitStack
 
 import concourse.mybir as mybir
 
-K, T, S, N, H, G, W = 512, 2048, 512, 512, 512, 2048, 256
+T, S, N, H, G, W = 2048, 512, 512, 512, 2048, 256
 FLOPS = 3 * 2 * 512 * 512 * 512
 
 F32 = mybir.dt.float32
@@ -18,12 +18,17 @@ ACT = mybir.ActivationFunctionType
 
 P = 128
 PACK = 4
-PIECES = ((0, 256), (256, 384), (384, 512))
-OUT_PIECES = ((0, 256), (256, 512))
+QUADRANTS = 4
+HALVES = ((0, W), (W, S))
+Z_PIECES = ((0, 256), (256, 384), (384, 512))
+SCALAR_TILES = (0, 1)
+VECTOR_TILES = (2, 3)
 
 
-def tile_picked_twkeycrossbratio_none_po_kernel(tc, x_words, x_scales, w1_words, w1_scales, d_words, d_scales, gn, w2_words, w2_scales,
-        offs, k1, two, n1, n2, n3, n4, out_0, out_1, out_2):
+def tile_picked_twkeycrossbratio_none_po_kernel(
+    tc, x_words, x_scales, w1_words, w1_scales, d_words, d_scales, gn, w2_words, w2_scales,
+    offs, k1, two, n1, n2, n3, n4, out_0, out_1, out_2,
+):
     nc = tc.nc
     with ExitStack() as ctx:
         lists = ctx.enter_context(tc.tile_pool(name="lists", bufs=1))
@@ -33,230 +38,225 @@ def tile_picked_twkeycrossbratio_none_po_kernel(tc, x_words, x_scales, w1_words,
         def tile(name, cols, dtype, tag=None):
             return sb.tile([P, cols], dtype, name=name, tag=tag or name, align_bytes=64)
 
+        def bank(number, cols):
+            return ps.tile([P, cols], F32, name="bank%d" % number)
+
+        def block(t):
+            return slice(t * W, (t + 1) * W)
+
+        def entries(index, lo, hi):
+            return index[:, lo // 16 : hi // 16]
+
+        def words_of(packed):
+            return packed[0].rearrange("p c r -> p (c r)").bitcast(I32)
+
         def load_list(name, src):
             dst = lists.tile([P, src.shape[1]], U16, name=name)
             nc.sync.dma_start(dst[:], src)
             return dst
 
-        def load_plane(queue, dst, src):
-            for q in range(4):
-                queue.dma_start(dst[32 * q : 32 * q + 4, :].bitcast(I32), src[0, 4 * q : 4 * q + 4, :].bitcast(I32))
+        def load_plane(dst, src):
+            for q in range(QUADRANTS):
+                nc.sync.dma_start(dst[32 * q : 32 * q + 4, :].bitcast(I32), src[0, 4 * q : 4 * q + 4, :].bitcast(I32))
 
-        def words_of(src):
-            return src[0].rearrange("p c r -> p (c r)").bitcast(I32)
+        def gather_words(dst, table, offsets):
+            nc.vector.tensor_copy(dst[:], table[:].bitcast(U32).indirect(offsets))
 
-        def gather_words(name, table, index, tag=None):
-            dst = tile(name, S, U32, tag)
-            nc.vector.tensor_copy(dst[:], table[:].bitcast(U32).indirect(index[:]))
-            return dst
+        def gather_bytes(dst, table, offsets):
+            nc.vector.tensor_copy(dst[:], table[:].indirect(offsets))
 
-        def gather_bytes(name, table, index, tag=None):
-            dst = tile(name, S, U8, tag)
-            nc.vector.tensor_copy(dst[:], table[:].indirect(index[:]))
-            return dst
-
-        def deal(name, src, width, tag=None):
-            dst = tile(name, src.shape[1], U8, tag)
+        def deal_bytes(name, src, width):
+            dst = tile(name, src.shape[1], U8)
             nc.vector.tensor_copy(
                 dst[:].rearrange("p (t m b) -> p t m b", t=PACK, b=width),
                 src[:].rearrange("p (m t b) -> p t m b", t=PACK, b=width),
             )
             return dst
 
-        xs = tile("xs", T, U8)
-        ds = tile("ds", G, U8)
-        w1s = tile("w1s", H, U8)
-        dp_s = tile("dp_s", H, U8)
-        nc.gpsimd.memset(xs[:, : T // 2].bitcast(I32), 0)
-        nc.vector.memset(xs[:, T // 2 :].bitcast(I32), 0)
-        for plane in (w1s, ds, dp_s):
-            nc.gpsimd.memset(plane[:].bitcast(I32), 0)
+        def product(out, lhsT, lhsT_scale, rhs, rhs_scale):
+            nc.tensor.matmul_mx(
+                out=out, lhsT=lhsT, lhsT_scale=lhsT_scale, rhs=rhs, rhs_scale=rhs_scale, start=True, stop=True
+            )
 
-        offs_l = load_list("offs_l", offs)
-        w1w = tile("w1w", 2 * H, U8, "staged")
-        nc.sync.dma_start(w1w[:].bitcast(I32), w1_words[0].bitcast(I32))
-        w2w = tile("w2w", 2 * N, U8)
-        nc.sync.dma_start(w2w[:].bitcast(I32), w2_words[0].bitcast(I32))
-        load_plane(nc.sync, xs, x_scales)
-        xw = tile("xw", T, I32)
-        nc.sync.dma_start(xw[:], words_of(x_words))
-        load_plane(nc.sync, w1s, w1_scales)
-        nc.sync.dma_start(ds[0:P:8, :].bitcast(I32), d_scales[0].bitcast(I32))
-        k1_l = load_list("k1_l", k1)
-        two_l = load_list("two_l", two)
-        w1w_d = deal("w1w_d", w1w, 2)
-        dw = tile("dw", G, I32, "staged")
-        nc.sync.dma_start(dw[:], words_of(d_words))
-        n1_l = load_list("n1_l", n1)
-        n2_l = load_list("n2_l", n2)
+        def fp4_columns(dealt_words, t):
+            return dealt_words[:, 2 * P * t : 2 * P * (t + 1)].bitcast(FP4X4)
+
+        x_bytes = tile("x_bytes", T, U8)
+        d_bytes = tile("d_bytes", G, U8)
+        w1_plane = tile("w1_plane", H, U8)
+        dk_plane = tile("dk_plane", H, U8)
+        nc.gpsimd.memset(x_bytes[:, : T // 2].bitcast(I32), 0)
+        nc.vector.memset(x_bytes[:, T // 2 :].bitcast(I32), 0)
+        for zeroed in (w1_plane, d_bytes, dk_plane):
+            nc.gpsimd.memset(zeroed[:].bitcast(I32), 0)
+
+        offs_list = load_list("offs_list", offs)
+        w1_raw = tile("w1_raw", 2 * H, U8, "staged")
+        nc.sync.dma_start(w1_raw[:].bitcast(I32), w1_words[0].bitcast(I32))
+        w2_raw = tile("w2_raw", 2 * N, U8)
+        nc.sync.dma_start(w2_raw[:].bitcast(I32), w2_words[0].bitcast(I32))
+        load_plane(x_bytes, x_scales)
+        x_table = tile("x_table", T, I32)
+        nc.sync.dma_start(x_table[:], words_of(x_words))
+        load_plane(w1_plane, w1_scales)
+        nc.sync.dma_start(d_bytes[0:P:8, :].bitcast(I32), d_scales[0].bitcast(I32))
+        k1_list = load_list("k1_list", k1)
+        two_list = load_list("two_list", two)
+        w1_dealt = deal_bytes("w1_dealt", w1_raw, 2)
+        d_table = tile("d_table", G, I32, "staged")
+        nc.sync.dma_start(d_table[:], words_of(d_words))
+        n1_list = load_list("n1_list", n1)
+        n2_list = load_list("n2_list", n2)
         gain = tile("gain", PACK, F32)
         nc.sync.dma_start(gain[:], gn.rearrange("(p t) o -> p (t o)", t=PACK))
-        n3_l = load_list("n3_l", n3)
-        n4_l = load_list("n4_l", n4)
+        n3_list = load_list("n3_list", n3)
+        n4_list = load_list("n4_list", n4)
 
         warm_in = tile("warm_in", 1, F32)
-        warm = tile("warm", 1, F32)
+        warm_out = tile("warm_out", 1, F32)
         nc.gpsimd.memset(warm_in[:], 1.0)
-        nc.scalar.activation(warm[:], warm_in[:], ACT.Abs_reciprocal_sqrt)
+        nc.scalar.activation(warm_out[:], warm_in[:], ACT.Abs_reciprocal_sqrt)
 
-        halves = ((0, W), (W, S))
-
-        def entries(index, lo, hi):
-            return index[:, lo // 16 : hi // 16]
-
-        def product(out, lhsT, lhsT_scale, rhs, rhs_scale):
-            nc.tensor.matmul_mx(out=out, lhsT=lhsT, lhsT_scale=lhsT_scale, rhs=rhs, rhs_scale=rhs_scale, start=True, stop=True)
-
-        w2w_d = deal("w2w_d", w2w, 2)
-        xq_s = gather_bytes("xq_s", xs, offs_l, "token_bytes")
-        y_sb = [tile("y_sb%d" % t, S, F32) for t in range(PACK)]
-        w1s_d = deal("w1s_d", w1s, 1)
-        for u, (lo, hi) in enumerate(halves):
-            xq_w = tile("xq_w%d" % u, W, U32, "token_words%d" % u)
-            nc.vector.tensor_copy(xq_w[:], xw[:].bitcast(U32).indirect(entries(offs_l, lo, hi)))
+        w2_dealt = deal_bytes("w2_dealt", w2_raw, 2)
+        xq_plane = tile("xq_plane", S, U8, "token_bytes")
+        gather_bytes(xq_plane, x_bytes, offs_list[:])
+        w1_plane_dealt = deal_bytes("w1_plane_dealt", w1_plane, 1)
+        y = [tile("y%d" % t, S, F32) for t in range(PACK)]
+        for u, (lo, hi) in enumerate(HALVES):
+            xq_words = tile("xq_words%d" % u, W, U32, "token_words%d" % u)
+            gather_words(xq_words, x_table, entries(offs_list, lo, hi))
             for t in range(PACK):
-                y_ps = ps.tile([P, W], F32, name="bank%d" % (PACK * u + t))
-                product(y_ps[:], w1w_d[:, 2 * P * t : 2 * P * (t + 1)].bitcast(FP4X4), w1s_d[:, P * t : P * (t + 1)],
-                        xq_w[:].bitcast(FP8X4), xq_s[:, lo:hi])
-                nc.scalar.copy(y_sb[t][:, lo:hi], y_ps[:])
-        y_n1 = {}
+                y_bank = bank(PACK * u + t, W)
+                product(y_bank[:], fp4_columns(w1_dealt, t), w1_plane_dealt[:, P * t : P * (t + 1)],
+                        xq_words[:].bitcast(FP8X4), xq_plane[:, lo:hi])
+                nc.scalar.copy(y[t][:, lo:hi], y_bank[:])
+        y_n1 = [tile("y_n1_first", PACK * W, F32)]
+        for t in range(PACK):
+            nc.scalar.activation(y_n1[0][:, block(t)], y[t][:].indirect(entries(n1_list, *HALVES[0])), ACT.Copy)
 
-        def fetch_y(t, u, dst):
-            y_n1[t, u] = dst
-            nc.scalar.activation(dst, y_sb[t][:].indirect(entries(n1_l, *halves[u])), ACT.Copy)
-
-        early = 4
-        y_early = tile("y_early", early * W, F32)
-        for e in range(early):
-            fetch_y(e % PACK, e // PACK, y_early[:, e * W : (e + 1) * W])
-        dg_s = gather_bytes("dg_s", ds, k1_l, "w1s")
-        dd_s = deal("dd_s", dg_s, 1)
+        dk_bytes = tile("dk_bytes", H, U8, "w1_plane")
+        gather_bytes(dk_bytes, d_bytes, k1_list[:])
+        dk_bytes_dealt = deal_bytes("dk_bytes_dealt", dk_bytes, 1)
         for r in range(4):
-            nc.sync.dma_start(dp_s[r:P:32, :].bitcast(I32), dd_s[8 * r : P : 32, :].bitcast(I32))
-        w2s = tile("w2s", N, U8, "dd_s")
-        nc.gpsimd.memset(w2s[:].bitcast(I32), 0)
-        load_plane(nc.sync, w2s, w2_scales)
-        dg_w = gather_words("dg_w", dw, k1_l)
-        dd_w = tile("dd_w", H, U32)
-        nc.vector.tensor_copy(dd_w[:].rearrange("p (t m) -> p m t", t=PACK), dg_w[:].rearrange("p (m t) -> p m t", t=PACK))
+            nc.sync.dma_start(dk_plane[r:P:32, :].bitcast(I32), dk_bytes_dealt[8 * r : P : 32, :].bitcast(I32))
+        w2_plane = tile("w2_plane", N, U8, "dk_bytes_dealt")
+        nc.gpsimd.memset(w2_plane[:].bitcast(I32), 0)
+        load_plane(w2_plane, w2_scales)
+        dk_words = tile("dk_words", H, U32)
+        gather_words(dk_words, d_table, k1_list[:])
+        dk_dealt = tile("dk_dealt", H, U32)
+        nc.vector.tensor_copy(
+            dk_dealt[:].rearrange("p (t m i) -> p m t i", t=PACK, i=4),
+            dk_words[:].rearrange("p (m i t) -> p m t i", t=PACK, i=4),
+        )
         factor = tile("factor", PACK, F32)
         nc.gpsimd.tensor_scalar(factor[:], gain[:], 0.75 * 0.0625, 0.0, ALU.mult, ALU.add)
-        d_sb = [tile("d_sb%d" % t, S, F32) for t in range(PACK)]
-        for u, (lo, hi) in enumerate(halves):
-            xt_w = tile("xt_w%d" % u, W, U32, ("token_words0", "dg_w")[u])
-            xt_s = tile("xt_s%d" % u, W, U8, ("token_bytes", "staged")[u])
-            nc.vector.tensor_copy(xt_w[:], xw[:].bitcast(U32).indirect(entries(two_l, lo, hi)))
-            nc.vector.tensor_copy(xt_s[:], xs[:].indirect(entries(two_l, lo, hi)))
+        d = [tile("d%d" % t, S, F32) for t in range(PACK)]
+        word_tags = ("token_words0", "dk_words")
+        byte_tags = ("token_bytes", "staged")
+        for u, (lo, hi) in enumerate(HALVES):
+            xt_words = tile("xt_words%d" % u, W, U32, word_tags[u])
+            xt_plane = tile("xt_plane%d" % u, W, U8, byte_tags[u])
+            gather_words(xt_words, x_table, entries(two_list, lo, hi))
+            gather_bytes(xt_plane, x_bytes, entries(two_list, lo, hi))
             for t in range(PACK):
-                d_ps = ps.tile([P, W], F32, name="bank%d" % (PACK * u + t))
-                product(d_ps[:], dd_w[:, P * t : P * (t + 1)].bitcast(FP8X4), dp_s[:, P * t : P * (t + 1)],
-                        xt_w[:].bitcast(FP8X4), xt_s[:])
-                nc.scalar.activation(d_sb[t][:, lo:hi], d_ps[:], ACT.Copy, scale=factor[:, t : t + 1])
-        w2s_d = deal("w2s_d", w2s, 1)
+                d_bank = bank(PACK * u + t, W)
+                product(d_bank[:], dk_dealt[:, P * t : P * (t + 1)].bitcast(FP8X4), dk_plane[:, P * t : P * (t + 1)],
+                        xt_words[:].bitcast(FP8X4), xt_plane[:])
+                nc.scalar.activation(d[t][:, lo:hi], d_bank[:], ACT.Copy, scale=factor[:, t : t + 1])
+        w2_plane_dealt = deal_bytes("w2_plane_dealt", w2_plane, 1)
 
-        y_late = tile("y_late", PACK * S, F32, "dg_w")
-        d_n2 = tile("d_n2", PACK * S, F32)
-        fused = 4
-        spans = ((0, 256), (256, 512))
-        for lo, hi in spans:
-            for t in range(PACK):
-                if lo >= W:
-                    nc.scalar.activation(y_late[:, S * t + lo : S * t + hi], y_sb[t][:].indirect(entries(n1_l, lo, hi)), ACT.Copy)
-                if not (lo == 0 and t < fused):
-                    nc.scalar.activation(d_n2[:, S * t + lo : S * t + hi], d_sb[t][:].indirect(entries(n2_l, lo, hi)), ACT.Copy)
+        y_n1.append(tile("y_n1_second", PACK * W, F32, "dk_words"))
+        d_n2_second = tile("d_n2_second", PACK * W, F32)
+        for t in range(PACK):
+            nc.scalar.activation(y_n1[1][:, block(t)], y[t][:].indirect(entries(n1_list, *HALVES[1])), ACT.Copy)
+            nc.scalar.activation(d_n2_second[:, block(t)], d[t][:].indirect(entries(n2_list, *HALVES[1])), ACT.Copy)
 
-        h_sb = [tile("h_sb%d" % t, S, F32) for t in range(PACK)]
-        for lo, hi in spans:
-            width = hi - lo
-            left = tile("left%d" % lo, PACK * width, F32)
-            right = tile("right%d" % lo, PACK * width, F32)
+        h = [tile("h%d" % t, S, F32) for t in range(PACK)]
+        for u, (lo, hi) in enumerate(HALVES):
+            left = tile("left%d" % u, PACK * W, F32)
+            right = tile("right%d" % u, PACK * W, F32)
             for t in range(PACK):
-                y_at = y_n1[t, 0] if lo == 0 else y_late[:, S * t + lo : S * t + hi]
-                nc.vector.tensor_tensor(right[:, width * t : width * (t + 1)], y_at, d_sb[t][:, lo:hi], ALU.mult)
+                nc.vector.tensor_tensor(right[:, block(t)], y_n1[u][:, block(t)], d[t][:, lo:hi], ALU.mult)
             for t in range(PACK):
-                if lo == 0 and t < fused:
-                    looked = d_sb[t][:].indirect(entries(n2_l, lo, hi))
-                else:
-                    looked = d_n2[:, S * t + lo : S * t + hi]
-                nc.vector.tensor_tensor(left[:, width * t : width * (t + 1)], looked, y_sb[t][:, lo:hi], ALU.mult)
-            pieces = [(a, b) for a, b in PIECES if lo <= a < hi]
-            z = {}
+                d_n2 = d_n2_second[:, block(t)] if u else d[t][:].indirect(entries(n2_list, lo, hi))
+                nc.vector.tensor_tensor(left[:, block(t)], d_n2, y[t][:, lo:hi], ALU.mult)
+            pieces = [(a, b) for a, b in Z_PIECES if lo <= a < hi]
+            z, z_words, z_plane = {}, {}, {}
             for a, b in pieces:
                 z[a] = tile("z%d" % a, PACK * (b - a), BF16)
-                cols = slice((a - lo) // 4, (b - lo) // 4)
+                column_pairs = slice((a - lo) // 2, (b - lo) // 2)
                 nc.vector.tensor_tensor(
-                    z[a][:].rearrange("p (c i t) -> p c t i", i=4, t=PACK),
-                    left[:].rearrange("p (t c i) -> p c t i", i=4, t=PACK)[:, cols],
-                    right[:].rearrange("p (t c i) -> p c t i", i=4, t=PACK)[:, cols],
+                    z[a][:].rearrange("p (c i t) -> p c t i", i=2, t=PACK),
+                    left[:].rearrange("p (t c i) -> p c t i", i=2, t=PACK)[:, column_pairs],
+                    right[:].rearrange("p (t c i) -> p c t i", i=2, t=PACK)[:, column_pairs],
                     ALU.subtract,
                 )
             for a, b in pieces:
-                z_w = tile("z_w%d" % a, b - a, U32)
-                z_s = tile("z_s%d" % a, b - a, U8)
-                nc.vector.quantize_mx(out=z_w[:].bitcast(FP8X4), scales=z_s[:], in_=z[a][:])
-                first_bank = PACK * (PIECES.index((a, b)) % 2)
-                h_ps = [ps.tile([P, b - a], F32, name="bank%d" % (first_bank + t)) for t in range(PACK)]
-                for t in range(PACK):
-                    product(h_ps[t][:], w2w_d[:, 2 * P * t : 2 * P * (t + 1)].bitcast(FP4X4), w2s_d[:, P * t : P * (t + 1)],
-                            z_w[:].bitcast(FP8X4), z_s[:])
-                    if a >= 256 and t % 2 == 1:
-                        nc.vector.tensor_copy(h_sb[t][:, a:b], h_ps[t][:])
+                z_words[a] = tile("z_words%d" % a, b - a, U32)
+                z_plane[a] = tile("z_plane%d" % a, b - a, U8)
+                nc.vector.quantize_mx(out=z_words[a][:].bitcast(FP8X4), scales=z_plane[a][:], in_=z[a][:])
+            for t in range(PACK):
+                for a, b in pieces:
+                    h_bank = bank(PACK * (Z_PIECES.index((a, b)) % 2) + t, b - a)
+                    product(h_bank[:], fp4_columns(w2_dealt, t), w2_plane_dealt[:, P * t : P * (t + 1)],
+                            z_words[a][:].bitcast(FP8X4), z_plane[a][:])
+                    if u and t % 2:
+                        nc.vector.tensor_copy(h[t][:, a:b], h_bank[:])
                     else:
-                        nc.scalar.copy(h_sb[t][:, a:b], h_ps[t][:])
+                        nc.scalar.copy(h[t][:, a:b], h_bank[:])
 
-        def part(t):
-            return slice(t * W, (t + 1) * W)
-
-        out_rows = out_0.rearrange("(p t) c -> p t c", t=PACK)
         pa = tile("pa", PACK * W, F32)
         pb = tile("pb", PACK * W, F32)
         size = tile("size", PACK * W, F32)
         root = tile("root", PACK * W, F32)
-        inv = tile("inv", PACK * W, F32)
+        inverse = tile("inverse", PACK * W, F32)
         rb = tile("rb", PACK * W, F32)
-        ra = tile("ra", 2 * W, F32)
-        res = [tile("res%d" % t, S, F32) for t in range(PACK)]
+        ra = tile("ra", len(SCALAR_TILES) * W, F32)
+        result = [tile("result%d" % t, S, F32) for t in range(PACK)]
         for t in range(PACK):
-            nc.scalar.activation(pb[:, part(t)], h_sb[t][:].indirect(n4_l[:]), ACT.Copy)
-            nc.vector.tensor_copy(pa[:, part(t)], h_sb[t][:].indirect(n3_l[:]))
-        sides = (slice(0, 2 * W), slice(2 * W, 4 * W))
-        for side in sides:
-            nc.scalar.activation(size[:, side], pb[:, side], ACT.Abs)
-        for side in sides:
-            nc.scalar.activation(root[:, side], size[:, side], ACT.Abs_reciprocal_sqrt, bias=0.5)
-        for side in sides:
-            nc.scalar.activation(inv[:, side], root[:, side], ACT.Square)
-        for side in sides:
-            nc.vector.tensor_tensor(rb[:, side], pa[:, side], pb[:, side], ALU.max)
-        nc.vector.tensor_tensor(ra[:], pa[:, sides[0]], inv[:, sides[0]], ALU.mult)
-        for t in range(PACK):
-            if t >= 2:
-                nc.vector.tensor_copy(res[t][:].indirect(n4_l[:]), rb[:, part(t)])
-            else:
-                nc.scalar.activation(res[t][:].indirect(n4_l[:]), rb[:, part(t)], ACT.Copy)
-        for t in range(PACK):
-            if t >= 2:
-                nc.vector.tensor_tensor(res[t][:].indirect(n3_l[:]), pa[:, part(t)], inv[:, part(t)], ALU.mult)
-            else:
-                nc.scalar.activation(res[t][:].indirect(n3_l[:]), ra[:, part(t)], ACT.Copy)
-            nc.sync.dma_start(out_rows[:, t, :], res[t][:])
-        pairs = [tile("pairs%d" % u, PACK * (hi - lo), BF16) for u, (lo, hi) in enumerate(OUT_PIECES)]
-        for t in (2, 3, 0, 1):
-            for u, (lo, hi) in enumerate(OUT_PIECES):
+            nc.scalar.activation(pb[:, block(t)], h[t][:].indirect(n4_list[:]), ACT.Copy)
+            nc.vector.tensor_copy(pa[:, block(t)], h[t][:].indirect(n3_list[:]))
+        scalar_part = slice(0, len(SCALAR_TILES) * W)
+        vector_part = slice(len(SCALAR_TILES) * W, PACK * W)
+        for part in (scalar_part, vector_part):
+            nc.scalar.activation(size[:, part], pb[:, part], ACT.Abs)
+        for part in (scalar_part, vector_part):
+            nc.scalar.activation(root[:, part], size[:, part], ACT.Abs_reciprocal_sqrt, bias=0.5)
+        for part in (scalar_part, vector_part):
+            nc.scalar.activation(inverse[:, part], root[:, part], ACT.Square)
+        for part in [scalar_part] + [block(t) for t in VECTOR_TILES]:
+            nc.vector.tensor_tensor(rb[:, part], pa[:, part], pb[:, part], ALU.max)
+        nc.vector.tensor_tensor(ra[:], pa[:, scalar_part], inverse[:, scalar_part], ALU.mult)
+        for t in SCALAR_TILES:
+            nc.scalar.activation(result[t][:].indirect(n4_list[:]), rb[:, block(t)], ACT.Copy)
+        for t in VECTOR_TILES:
+            nc.vector.tensor_copy(result[t][:].indirect(n4_list[:]), rb[:, block(t)])
+        out_rows = out_0.rearrange("(p t) c -> p t c", t=PACK)
+        for t in SCALAR_TILES:
+            nc.scalar.activation(result[t][:].indirect(n3_list[:]), ra[:, block(t)], ACT.Copy)
+            nc.sync.dma_start(out_rows[:, t, :], result[t][:])
+        for t in VECTOR_TILES:
+            nc.vector.tensor_tensor(result[t][:].indirect(n3_list[:]), pa[:, block(t)], inverse[:, block(t)], ALU.mult)
+            nc.sync.dma_start(out_rows[:, t, :], result[t][:])
+
+        pairs = [tile("pairs%d" % u, PACK * W, BF16) for u in range(len(HALVES))]
+        for t in VECTOR_TILES + SCALAR_TILES:
+            for u, (lo, hi) in enumerate(HALVES):
                 nc.vector.tensor_copy(
-                    pairs[u][:].rearrange("p (v c e) -> p v c e", v=2, e=2)[:, t // 2, :, t % 2], res[t][:, lo:hi]
+                    pairs[u][:].rearrange("p (v c e) -> p v c e", v=2, e=2)[:, t // 2, :, t % 2], result[t][:, lo:hi]
                 )
-        grouped = [tile("grouped%d" % u, PACK * (hi - lo), BF16) for u, (lo, hi) in enumerate(OUT_PIECES)]
-        for u in range(len(OUT_PIECES)):
+        grouped = [tile("grouped%d" % u, PACK * W, BF16) for u in range(len(HALVES))]
+        for u in range(len(HALVES)):
             nc.vector.tensor_copy(
                 grouped[u][:].bitcast(I32).rearrange("p (c v) -> p c v", v=2),
                 pairs[u][:].bitcast(I32).rearrange("p (v c) -> p c v", v=2),
             )
-        o_w = tile("o_w", S, I32)
-        o_s = tile("o_s", S, U8)
-        for u, (lo, hi) in enumerate(OUT_PIECES):
-            nc.vector.quantize_mx(out=o_w[:, lo:hi].bitcast(FP8X4), scales=o_s[:, lo:hi], in_=grouped[u][:])
-            nc.sync.dma_start(words_of(out_1)[:, lo:hi], o_w[:, lo:hi])
-        for q in range(4):
-            queue = nc.scalar if q % 2 == 0 else nc.sync
-            queue.dma_start(out_2[0, 4 * q : 4 * q + 4, :].bitcast(I32), o_s[32 * q : 32 * q + 4, :].bitcast(I32))
+        out_words = tile("out_words", S, I32)
+        out_plane = tile("out_plane", S, U8)
+        for u, (lo, hi) in enumerate(HALVES):
+            nc.vector.quantize_mx(out=out_words[:, lo:hi].bitcast(FP8X4), scales=out_plane[:, lo:hi], in_=grouped[u][:])
+            nc.sync.dma_start(words_of(out_1)[:, lo:hi], out_words[:, lo:hi])
+        for q in range(QUADRANTS):
+            queue = nc.sync if q % 2 else nc.scalar
+            queue.dma_start(out_2[0, 4 * q : 4 * q + 4, :].bitcast(I32), out_plane[32 * q : 32 * q + 4, :].bitcast(I32))

@@ -91,7 +91,7 @@ def tile_picked_twkeycrossbratio_none_po_kernel(
             nc.gpsimd.memset(zeroed[:].bitcast(I32), 0)
 
         offs_list = load_list("offs_list", offs)
-        w1_raw = tile("w1_raw", 2 * H, U8, "staged")
+        w1_raw = tile("w1_raw", 2 * H, U8)
         nc.sync.dma_start(w1_raw[:].bitcast(I32), w1_words[0].bitcast(I32))
         w2_raw = tile("w2_raw", 2 * N, U8)
         nc.sync.dma_start(w2_raw[:].bitcast(I32), w2_words[0].bitcast(I32))
@@ -101,10 +101,9 @@ def tile_picked_twkeycrossbratio_none_po_kernel(
         load_plane(w1_plane, w1_scales)
         nc.sync.dma_start(d_bytes[0:P:8, :].bitcast(I32), d_scales[0].bitcast(I32))
         k1_list = load_list("k1_list", k1)
-        two_list = load_list("two_list", two)
-        w1_dealt = deal_bytes("w1_dealt", w1_raw, 2)
-        d_table = tile("d_table", G, I32, "staged")
+        d_table = tile("d_table", G, I32)
         nc.sync.dma_start(d_table[:], words_of(d_words))
+        two_list = load_list("two_list", two)
         n1_list = load_list("n1_list", n1)
         n2_list = load_list("n2_list", n2)
         gain = tile("gain", PACK, F32)
@@ -117,21 +116,20 @@ def tile_picked_twkeycrossbratio_none_po_kernel(
         nc.gpsimd.memset(warm_in[:], 1.0)
         nc.scalar.activation(warm_out[:], warm_in[:], ACT.Abs_reciprocal_sqrt)
 
+        w1_dealt = deal_bytes("w1_dealt", w1_raw, 2)
         w2_dealt = deal_bytes("w2_dealt", w2_raw, 2)
-        xq_plane = tile("xq_plane", S, U8, "token_bytes")
+        xq_plane = tile("xq_plane", S, U8)
         gather_bytes(xq_plane, x_bytes, offs_list[:])
+        xq_words = tile("xq_words", S, U32)
+        gather_words(xq_words, x_table, offs_list[:])
         w1_plane_dealt = deal_bytes("w1_plane_dealt", w1_plane, 1)
         y = [tile("y%d" % t, S, F32) for t in range(PACK)]
-        for u, (lo, hi) in enumerate(HALVES):
-            xq_words = tile("xq_words%d" % u, W, U32, "token_words%d" % u)
-            gather_words(xq_words, x_table, entries(offs_list, lo, hi))
-            for t in range(PACK):
-                y_bank = bank(PACK * u + t, W)
-                product(y_bank[:], fp4_columns(w1_dealt, t), w1_plane_dealt[:, P * t : P * (t + 1)],
-                        xq_words[:].bitcast(FP8X4), xq_plane[:, lo:hi])
-                nc.scalar.copy(y[t][:, lo:hi], y_bank[:])
         y_n1 = [tile("y_n1_first", PACK * W, F32)]
         for t in range(PACK):
+            y_bank = bank(t, S)
+            product(y_bank[:], fp4_columns(w1_dealt, t), w1_plane_dealt[:, P * t : P * (t + 1)],
+                    xq_words[:].bitcast(FP8X4), xq_plane[:])
+            nc.scalar.copy(y[t][:], y_bank[:])
             nc.scalar.activation(y_n1[0][:, block(t)], y[t][:].indirect(entries(n1_list, *HALVES[0])), ACT.Copy)
 
         dk_bytes = tile("dk_bytes", H, U8, "w1_plane")
@@ -152,15 +150,15 @@ def tile_picked_twkeycrossbratio_none_po_kernel(
         factor = tile("factor", PACK, F32)
         nc.gpsimd.tensor_scalar(factor[:], gain[:], 0.75 * 0.0625, 0.0, ALU.mult, ALU.add)
         d = [tile("d%d" % t, S, F32) for t in range(PACK)]
-        word_tags = ("token_words0", "dk_words")
-        byte_tags = ("token_bytes", "staged")
+        word_tags = ("xq_words", "dk_words")
+        byte_tags = ("xq_plane", "d_table")
         for u, (lo, hi) in enumerate(HALVES):
             xt_words = tile("xt_words%d" % u, W, U32, word_tags[u])
             xt_plane = tile("xt_plane%d" % u, W, U8, byte_tags[u])
             gather_words(xt_words, x_table, entries(two_list, lo, hi))
             gather_bytes(xt_plane, x_bytes, entries(two_list, lo, hi))
             for t in range(PACK):
-                d_bank = bank(PACK * u + t, W)
+                d_bank = bank(PACK * (1 - u) + t, W)
                 product(d_bank[:], dk_dealt[:, P * t : P * (t + 1)].bitcast(FP8X4), dk_plane[:, P * t : P * (t + 1)],
                         xt_words[:].bitcast(FP8X4), xt_plane[:])
                 nc.scalar.activation(d[t][:, lo:hi], d_bank[:], ACT.Copy, scale=factor[:, t : t + 1])

from contextlib import ExitStack

import concourse.mybir as mybir

T, S, N, H, G, W = 2048, 512, 512, 512, 2048, 256
FLOPS = 3 * 2 * 512 * 512 * 512

F32 = mybir.dt.float32
BF16 = mybir.dt.bfloat16
I32 = mybir.dt.int32
U32 = mybir.dt.uint32
U16 = mybir.dt.uint16
U8 = mybir.dt.uint8
FP8X4 = mybir.dt.float8_e4m3fn_x4
FP4X4 = mybir.dt.float4_e2m1fn_x4
ALU = mybir.AluOpType
ACT = mybir.ActivationFunctionType

P = 128
PACK = 4
QUADRANTS = 4
HALVES = ((0, W), (W, S))
Z_PIECES = ((0, 256), (256, 384), (384, 512))
SCALAR_TILES = (0, 1)
VECTOR_TILES = (2, 3)


def tile_picked_twkeycrossbratio_none_po_kernel(
    tc, x_words, x_scales, w1_words, w1_scales, d_words, d_scales, gn, w2_words, w2_scales,
    offs, k1, two, n1, n2, n3, n4, out_0, out_1, out_2,
):
    nc = tc.nc
    with ExitStack() as ctx:
        lists = ctx.enter_context(tc.tile_pool(name="lists", bufs=1))
        sb = ctx.enter_context(tc.tile_pool(name="sb", bufs=1))
        ps = ctx.enter_context(tc.psum_pool(name="ps", bufs=1))

        def tile(name, cols, dtype, tag=None):
            return sb.tile([P, cols], dtype, name=name, tag=tag or name, align_bytes=64)

        def bank(number, cols):
            return ps.tile([P, cols], F32, name="bank%d" % number)

        def block(t):
            return slice(t * W, (t + 1) * W)

        def entries(index, lo, hi):
            return index[:, lo // 16 : hi // 16]

        def words_of(packed):
            return packed[0].rearrange("p c r -> p (c r)").bitcast(I32)

        def load_list(name, src):
            dst = lists.tile([P, src.shape[1]], U16, name=name)
            nc.sync.dma_start(dst[:], src)
            return dst

        def load_plane(dst, src):
            for q in range(QUADRANTS):
                nc.sync.dma_start(dst[32 * q : 32 * q + 4, :].bitcast(I32), src[0, 4 * q : 4 * q + 4, :].bitcast(I32))

        def gather_words(dst, table, offsets):
            nc.vector.tensor_copy(dst[:], table[:].bitcast(U32).indirect(offsets))

        def gather_bytes(dst, table, offsets):
            nc.vector.tensor_copy(dst[:], table[:].indirect(offsets))

        def deal_bytes(name, src, width):
            dst = tile(name, src.shape[1], U8)
            nc.vector.tensor_copy(
                dst[:].rearrange("p (t m b) -> p t m b", t=PACK, b=width),
                src[:].rearrange("p (m t b) -> p t m b", t=PACK, b=width),
            )
            return dst

        def product(out, lhsT, lhsT_scale, rhs, rhs_scale):
            nc.tensor.matmul_mx(
                out=out, lhsT=lhsT, lhsT_scale=lhsT_scale, rhs=rhs, rhs_scale=rhs_scale, start=True, stop=True
            )

        def fp4_columns(dealt_words, t):
            return dealt_words[:, 2 * P * t : 2 * P * (t + 1)].bitcast(FP4X4)

        x_bytes = tile("x_bytes", T, U8)
        d_bytes = tile("d_bytes", G, U8)
        w1_plane = tile("w1_plane", H, U8)
        dk_plane = tile("dk_plane", H, U8)
        nc.gpsimd.memset(x_bytes[:, : T // 2].bitcast(I32), 0)
        nc.vector.memset(x_bytes[:, T // 2 :].bitcast(I32), 0)
        for zeroed in (w1_plane, d_bytes, dk_plane):
            nc.gpsimd.memset(zeroed[:].bitcast(I32), 0)

        offs_list = load_list("offs_list", offs)
        w1_raw = tile("w1_raw", 2 * H, U8)
        nc.sync.dma_start(w1_raw[:].bitcast(I32), w1_words[0].bitcast(I32))
        w2_raw = tile("w2_raw", 2 * N, U8)
        nc.sync.dma_start(w2_raw[:].bitcast(I32), w2_words[0].bitcast(I32))
        load_plane(x_bytes, x_scales)
        x_table = tile("x_table", T, I32)
        nc.sync.dma_start(x_table[:], words_of(x_words))
        load_plane(w1_plane, w1_scales)
        nc.sync.dma_start(d_bytes[0:P:8, :].bitcast(I32), d_scales[0].bitcast(I32))
        k1_list = load_list("k1_list", k1)
        d_table = tile("d_table", G, I32)
        nc.sync.dma_start(d_table[:], words_of(d_words))
        two_list = load_list("two_list", two)
        n1_list = load_list("n1_list", n1)
        n2_list = load_list("n2_list", n2)
        gain = tile("gain", PACK, F32)
        nc.sync.dma_start(gain[:], gn.rearrange("(p t) o -> p (t o)", t=PACK))
        n3_list = load_list("n3_list", n3)
        n4_list = load_list("n4_list", n4)

        warm_in = tile("warm_in", 1, F32)
        warm_out = tile("warm_out", 1, F32)
        nc.gpsimd.memset(warm_in[:], 1.0)
        nc.scalar.activation(warm_out[:], warm_in[:], ACT.Abs_reciprocal_sqrt)

        w1_dealt = deal_bytes("w1_dealt", w1_raw, 2)
        w2_dealt = deal_bytes("w2_dealt", w2_raw, 2)
        xq_plane = tile("xq_plane", S, U8)
        gather_bytes(xq_plane, x_bytes, offs_list[:])
        xq_words = tile("xq_words", S, U32)
        gather_words(xq_words, x_table, offs_list[:])
        w1_plane_dealt = deal_bytes("w1_plane_dealt", w1_plane, 1)
        y = [tile("y%d" % t, S, F32) for t in range(PACK)]
        y_n1 = [tile("y_n1_first", PACK * W, F32)]
        for t in range(PACK):
            y_bank = bank(t, S)
            product(y_bank[:], fp4_columns(w1_dealt, t), w1_plane_dealt[:, P * t : P * (t + 1)],
                    xq_words[:].bitcast(FP8X4), xq_plane[:])
            nc.scalar.copy(y[t][:], y_bank[:])
            nc.scalar.activation(y_n1[0][:, block(t)], y[t][:].indirect(entries(n1_list, *HALVES[0])), ACT.Copy)

        dk_bytes = tile("dk_bytes", H, U8, "w1_plane")
        gather_bytes(dk_bytes, d_bytes, k1_list[:])
        dk_bytes_dealt = deal_bytes("dk_bytes_dealt", dk_bytes, 1)
        for r in range(4):
            nc.sync.dma_start(dk_plane[r:P:32, :].bitcast(I32), dk_bytes_dealt[8 * r : P : 32, :].bitcast(I32))
        w2_plane = tile("w2_plane", N, U8, "dk_bytes_dealt")
        nc.gpsimd.memset(w2_plane[:].bitcast(I32), 0)
        load_plane(w2_plane, w2_scales)
        dk_words = tile("dk_words", H, U32)
        gather_words(dk_words, d_table, k1_list[:])
        dk_dealt = tile("dk_dealt", H, U32)
        nc.vector.tensor_copy(
            dk_dealt[:].rearrange("p (t m i) -> p m t i", t=PACK, i=4),
            dk_words[:].rearrange("p (m i t) -> p m t i", t=PACK, i=4),
        )
        factor = tile("factor", PACK, F32)
        nc.gpsimd.tensor_scalar(factor[:], gain[:], 0.75 * 0.0625, 0.0, ALU.mult, ALU.add)
        d = [tile("d%d" % t, S, F32) for t in range(PACK)]
        word_tags = ("xq_words", "dk_words")
        byte_tags = ("xq_plane", "d_table")
        for u, (lo, hi) in enumerate(HALVES):
            xt_words = tile("xt_words%d" % u, W, U32, word_tags[u])
            xt_plane = tile("xt_plane%d" % u, W, U8, byte_tags[u])
            gather_words(xt_words, x_table, entries(two_list, lo, hi))
            gather_bytes(xt_plane, x_bytes, entries(two_list, lo, hi))
            for t in range(PACK):
                d_bank = bank(PACK * (1 - u) + t, W)
                product(d_bank[:], dk_dealt[:, P * t : P * (t + 1)].bitcast(FP8X4), dk_plane[:, P * t : P * (t + 1)],
                        xt_words[:].bitcast(FP8X4), xt_plane[:])
                nc.scalar.activation(d[t][:, lo:hi], d_bank[:], ACT.Copy, scale=factor[:, t : t + 1])
        w2_plane_dealt = deal_bytes("w2_plane_dealt", w2_plane, 1)

        y_n1.append(tile("y_n1_second", PACK * W, F32, "dk_words"))
        d_n2_second = tile("d_n2_second", PACK * W, F32)
        for t in range(PACK):
            nc.scalar.activation(y_n1[1][:, block(t)], y[t][:].indirect(entries(n1_list, *HALVES[1])), ACT.Copy)
            nc.scalar.activation(d_n2_second[:, block(t)], d[t][:].indirect(entries(n2_list, *HALVES[1])), ACT.Copy)

        h = [tile("h%d" % t, S, F32) for t in range(PACK)]
        for u, (lo, hi) in enumerate(HALVES):
            left = tile("left%d" % u, PACK * W, F32)
            right = tile("right%d" % u, PACK * W, F32)
            for t in range(PACK):
                nc.vector.tensor_tensor(right[:, block(t)], y_n1[u][:, block(t)], d[t][:, lo:hi], ALU.mult)
            for t in range(PACK):
                d_n2 = d_n2_second[:, block(t)] if u else d[t][:].indirect(entries(n2_list, lo, hi))
                nc.vector.tensor_tensor(left[:, block(t)], d_n2, y[t][:, lo:hi], ALU.mult)
            pieces = [(a, b) for a, b in Z_PIECES if lo <= a < hi]
            z, z_words, z_plane = {}, {}, {}
            for a, b in pieces:
                z[a] = tile("z%d" % a, PACK * (b - a), BF16)
                column_pairs = slice((a - lo) // 2, (b - lo) // 2)
                nc.vector.tensor_tensor(
                    z[a][:].rearrange("p (c i t) -> p c t i", i=2, t=PACK),
                    left[:].rearrange("p (t c i) -> p c t i", i=2, t=PACK)[:, column_pairs],
                    right[:].rearrange("p (t c i) -> p c t i", i=2, t=PACK)[:, column_pairs],
                    ALU.subtract,
                )
            for a, b in pieces:
                z_words[a] = tile("z_words%d" % a, b - a, U32)
                z_plane[a] = tile("z_plane%d" % a, b - a, U8)
                nc.vector.quantize_mx(out=z_words[a][:].bitcast(FP8X4), scales=z_plane[a][:], in_=z[a][:])
            for t in range(PACK):
                for a, b in pieces:
                    h_bank = bank(PACK * (Z_PIECES.index((a, b)) % 2) + t, b - a)
                    product(h_bank[:], fp4_columns(w2_dealt, t), w2_plane_dealt[:, P * t : P * (t + 1)],
                            z_words[a][:].bitcast(FP8X4), z_plane[a][:])
                    if u and t % 2:
                        nc.vector.tensor_copy(h[t][:, a:b], h_bank[:])
                    else:
                        nc.scalar.copy(h[t][:, a:b], h_bank[:])

        pa = tile("pa", PACK * W, F32)
        pb = tile("pb", PACK * W, F32)
        size = tile("size", PACK * W, F32)
        root = tile("root", PACK * W, F32)
        inverse = tile("inverse", PACK * W, F32)
        rb = tile("rb", PACK * W, F32)
        ra = tile("ra", len(SCALAR_TILES) * W, F32)
        result = [tile("result%d" % t, S, F32) for t in range(PACK)]
        for t in range(PACK):
            nc.scalar.activation(pb[:, block(t)], h[t][:].indirect(n4_list[:]), ACT.Copy)
            nc.vector.tensor_copy(pa[:, block(t)], h[t][:].indirect(n3_list[:]))
        scalar_part = slice(0, len(SCALAR_TILES) * W)
        vector_part = slice(len(SCALAR_TILES) * W, PACK * W)
        for part in (scalar_part, vector_part):
            nc.scalar.activation(size[:, part], pb[:, part], ACT.Abs)
        for part in (scalar_part, vector_part):
            nc.scalar.activation(root[:, part], size[:, part], ACT.Abs_reciprocal_sqrt, bias=0.5)
        for part in (scalar_part, vector_part):
            nc.scalar.activation(inverse[:, part], root[:, part], ACT.Square)
        for part in [scalar_part] + [block(t) for t in VECTOR_TILES]:
            nc.vector.tensor_tensor(rb[:, part], pa[:, part], pb[:, part], ALU.max)
        nc.vector.tensor_tensor(ra[:], pa[:, scalar_part], inverse[:, scalar_part], ALU.mult)
        for t in SCALAR_TILES:
            nc.scalar.activation(result[t][:].indirect(n4_list[:]), rb[:, block(t)], ACT.Copy)
        for t in VECTOR_TILES:
            nc.vector.tensor_copy(result[t][:].indirect(n4_list[:]), rb[:, block(t)])
        out_rows = out_0.rearrange("(p t) c -> p t c", t=PACK)
        for t in SCALAR_TILES:
            nc.scalar.activation(result[t][:].indirect(n3_list[:]), ra[:, block(t)], ACT.Copy)
            nc.sync.dma_start(out_rows[:, t, :], result[t][:])
        for t in VECTOR_TILES:
            nc.vector.tensor_tensor(result[t][:].indirect(n3_list[:]), pa[:, block(t)], inverse[:, block(t)], ALU.mult)
            nc.sync.dma_start(out_rows[:, t, :], result[t][:])

        pairs = [tile("pairs%d" % u, PACK * W, BF16) for u in range(len(HALVES))]
        for t in VECTOR_TILES + SCALAR_TILES:
            for u, (lo, hi) in enumerate(HALVES):
                nc.vector.tensor_copy(
                    pairs[u][:].rearrange("p (v c e) -> p v c e", v=2, e=2)[:, t // 2, :, t % 2], result[t][:, lo:hi]
                )
        grouped = [tile("grouped%d" % u, PACK * W, BF16) for u in range(len(HALVES))]
        for u in range(len(HALVES)):
            nc.vector.tensor_copy(
                grouped[u][:].bitcast(I32).rearrange("p (c v) -> p c v", v=2),
                pairs[u][:].bitcast(I32).rearrange("p (v c) -> p c v", v=2),
            )
        out_words = tile("out_words", S, I32)
        out_plane = tile("out_plane", S, U8)
        for u, (lo, hi) in enumerate(HALVES):
            nc.vector.quantize_mx(out=out_words[:, lo:hi].bitcast(FP8X4), scales=out_plane[:, lo:hi], in_=grouped[u][:])
            nc.sync.dma_start(words_of(out_1)[:, lo:hi], out_words[:, lo:hi])
        for q in range(QUADRANTS):
            queue = nc.sync if q % 2 else nc.scalar
            queue.dma_start(out_2[0, 4 * q : 4 * q + 4, :].bitcast(I32), out_plane[32 * q : 32 * q + 4, :].bitcast(I32))
